import numpy as np
import ml_dtypes


def mxq(x, axis, fmt="e4m3"):
    dtype, down = {"e4m3": (ml_dtypes.float8_e4m3fn, 7), "e5m2": (ml_dtypes.float8_e5m2, 14)}[fmt]
    v = np.moveaxis(np.asarray(x, np.float32).astype(ml_dtypes.bfloat16).astype(np.float64), axis, -1)
    blocks = v.reshape(v.shape[:-1] + (-1, 32))
    amax = np.abs(blocks).max(-1, keepdims=True)
    byte = np.maximum(np.where(amax > 0, np.frexp(amax)[1] - 1 + 127, 0) - down, 1)
    scale = np.exp2(byte - 127.0)
    codes = (blocks / scale).astype(np.float32).astype(dtype).astype(np.float64)
    return np.moveaxis((codes * scale).reshape(v.shape), -1, axis)


WIDE = False


def mx_kscale(k):
    if not WIDE:
        return np.ones(k)
    levels = np.array([10, -10, 5, -5, 0])
    if k % 512:
        return np.exp2(np.random.permutation(np.resize(levels, k // 32))).repeat(32)
    a = np.empty((k // 512, 16))
    for p in range(k // 512):
        a[p, :8] = np.random.permutation(np.resize(levels, 8))
        for g in range(8):
            far = levels[np.abs(levels - a[p, g]) >= 10]
            a[p, g + 8] = far[np.random.randint(len(far))]
    return np.exp2(a.ravel()).repeat(32)


def f64(x):
    return np.asarray(x).astype(np.float64)


def striped(idx):
    return np.tile(idx.reshape(-1, 16).T, (8, 1)).astype(np.uint16)


def unstriped(offs):
    return offs[:16].T.reshape(-1).astype(np.int64)


E2M1 = np.array([0.0, 0.5, 1.0, 1.5, 2.0, 3.0, 4.0, 6.0, -0.0, -0.5, -1.0, -1.5, -2.0, -3.0, -4.0, -6.0])


def pack_weight(w, fmt):
    k, n = w.shape
    w = f64(np.asarray(w, np.float32).astype(ml_dtypes.bfloat16)).reshape(k // 32, 32, n)
    amax = np.abs(w).max(1)
    if fmt == "e4m3":
        byte = np.frexp(amax)[1] - 1 + 127 - 7
    else:
        mant, ex = np.frexp(amax / 6.0)
        byte = np.where(mant > 0.5, ex, ex - 1) + 127
    byte = np.clip(np.where(amax > 0, byte, 1), 1, 254)
    scaled = (w * np.exp2(127.0 - byte)[:, None, :]).reshape(k, n).astype(np.float32)
    by_word = np.ascontiguousarray(scaled.reshape(k // 512, 128, 4, n).transpose(0, 1, 3, 2))
    if fmt == "e4m3":
        words = by_word.astype(ml_dtypes.float8_e4m3fn).view(np.uint8)
    else:
        c = by_word.astype(ml_dtypes.float4_e2m1fn).view(np.uint8) & 0xF
        words = (c[..., 0::2] | (c[..., 1::2] << 4)).reshape(k // 512, 128, 2 * n)
    return np.ascontiguousarray(words), np.ascontiguousarray(byte.astype(np.uint8).reshape(k // 512, 16, n))


def unpack_weight(words, scales, fmt):
    g, _, n = scales.shape
    words = np.ascontiguousarray(words).reshape(g, 128, n, -1)
    if fmt == "e4m3":
        vals = words.view(ml_dtypes.float8_e4m3fn).astype(np.float64)
    else:
        nib = np.empty((g, 128, n, 4), np.uint8)
        nib[..., 0::2] = words & 0xF
        nib[..., 1::2] = words >> 4
        vals = E2M1[nib]
    vals = vals * np.repeat(np.exp2(scales.astype(np.float64) - 127.0), 8, axis=1)[..., None]
    return vals.transpose(0, 1, 3, 2).reshape(g * 512, n)


def silu(v):
    return v / (1.0 + np.exp(-np.maximum(v, -700.0)))


K, T, E, C, N = 1536, 768, 12, 256, 128
TOP = 4


def by_expert(wq, xq):
    return np.concatenate([wq[e].T @ xq[:, e * C:(e + 1) * C] for e in range(E)], axis=1)


def setup_inputs():
    n = np.random.standard_normal
    s = mx_kscale(K)[:, None]
    deal = np.repeat(np.arange(E), C).reshape(TOP, T)[:, np.random.permutation(T)]
    deal = np.take_along_axis(deal, np.argsort(np.random.rand(TOP, T), axis=0), axis=0)
    for _ in range(8):
        s_, t_ = np.random.permutation(T).reshape(2, -1); r = np.random.randint(TOP, size=T // 2); x, y = deal[r, s_].copy(), deal[r, t_].copy()
        ok = ~((deal[:, s_] == y).any(0) | (deal[:, t_] == x).any(0)); deal[r[ok], s_[ok]] = y[ok]; deal[r[ok], t_[ok]] = x[ok]
    order = np.lexsort((np.random.rand(TOP * T), deal.reshape(-1)))
    slot_token = order % T; pos = np.empty(TOP * T, np.int64); pos[order] = np.arange(TOP * T); pos = pos.reshape(TOP, T)
    g = np.random.uniform(0.5, 1.5, (TOP, T)); g = g / g.sum(0)
    w = [pack_weight(m, "e2m1") for m in n((E, K, N)) / np.sqrt(K) / s[None]]
    w_slot = np.empty(E * C)
    for r in range(TOP): w_slot[pos[r]] = g[r]
    return {
        "xT": (n((K, T)) * s).astype(np.float32),
        "w_words": np.stack([m[0] for m in w]),
        "w_scales": np.stack([m[1] for m in w]),
        "b": (0.3 * n((N, E))).astype(np.float32),
        "gate": np.tile(w_slot, (K, 1)).astype(np.float32),
        "offs": striped(slot_token),
        "pos1": striped(pos[0]),
        "pos2": striped(pos[1]),
        "pos3": striped(pos[2]),
        "pos4": striped(pos[3]),
    }


def reference(xT, w_words, w_scales, b, gate, offs, pos1, pos2, pos3, pos4):
    idx = unstriped(offs)
    w = np.stack([unpack_weight(w_words[e], w_scales[e], "e2m1") for e in range(E)])
    xq = mxq(f64(gate) * f64(xT)[:, idx], 0, "e4m3")
    y = by_expert(w, xq)
    y = silu(y + np.repeat(f64(b), C, axis=1))
    return y[:, unstriped(pos1)] + y[:, unstriped(pos2)] + y[:, unstriped(pos3)] + y[:, unstriped(pos4)]

@@ -1,0 +1,202 @@
+from contextlib import ExitStack
+
+import concourse.mybir as mybir
+from concourse.masks import make_identity
+
+K, T, E, C, N = 1536, 768, 12, 256, 128
+SLOTS = E * C
+P = 128
+PACK = 4
+PASSES = K // (P * PACK)
+BLOCKS = SLOTS // P
+CHUNKS = (512, 512, 512, 512, 512, 256, 256)
+WIDEST = max(CHUNKS)
+TOKEN_CUTS = (384, 384)
+STAGES = 4
+IN_BANKS = 4
+OUT_BANKS = 4
+GATED_TILES = 4
+EXPERT_LAG = 4
+
+F32 = mybir.dt.float32
+BF16 = mybir.dt.bfloat16
+I32 = mybir.dt.int32
+U32 = mybir.dt.uint32
+U16 = mybir.dt.uint16
+U8 = mybir.dt.uint8
+FP8X4 = mybir.dt.float8_e4m3fn_x4
+FP4X4 = mybir.dt.float4_e2m1fn_x4
+ACT = mybir.ActivationFunctionType
+ADD = mybir.AluOpType.add
+
+FLOPS = 2 * K * N * SLOTS
+BYTES = 4 * K * T + E * K * N // 2 + E * K * N // 32 + 4 * N * E + 4 * SLOTS + 2 * P * (SLOTS + 4 * T) // 16 + 4 * N * T
+
+
+def tile_moe_pre_lin_silu_kernel(
+    tc, xT, w_words, w_scales, b, gate, offs, pos1, pos2, pos3, pos4, out
+):
+    nc = tc.nc
+    with ExitStack() as ctx:
+        keep = ctx.enter_context(tc.tile_pool(name="keep", bufs=1))
+        banks = ctx.enter_context(tc.psum_pool(name="banks", bufs=1))
+
+        slot_tokens = keep.tile([P, SLOTS // 16], U16, name="slot_tokens")
+        nc.sync.dma_start(slot_tokens[:], offs)
+
+        x_rows = xT.rearrange("(a p j) t -> a j p t", p=P, j=PACK)
+        x_planes = [[keep.tile([P, T], F32, name="x_%d_%d" % (a, j)) for j in range(PACK)] for a in range(PASSES)]
+
+        def load_pass(a):
+            for j in range(PACK):
+                nc.sync.dma_start(x_planes[a][j][:], x_rows[a, j])
+
+        ident = keep.tile([P, P], F32, name="ident")
+        make_identity(nc, ident[:])
+        gate_rows = keep.tile([P, P], F32, name="gate_rows")
+        nc.gpsimd.memset(gate_rows[:], 0.0)
+        w_scale = keep.tile([P, E * PASSES * N], U8, name="w_scale", align_bytes=64)
+        nc.gpsimd.memset(w_scale[:].bitcast(I32), 0)
+
+        load_pass(0)
+        nc.sync.dma_start(gate_rows[0:BLOCKS, :], gate[0].rearrange("(b s) -> b s", s=P))
+        load_pass(1)
+        load_pass(2)
+
+        w_code = keep.tile([P, E * PASSES, 2 * N], U8, name="w_code", align_bytes=64)
+        nc.sync.dma_start(w_code[:].bitcast(I32), w_words.rearrange("e a p b -> p (e a) b").bitcast(I32))
+        scale_rows = w_scales.rearrange("e a (q r) n -> r q (e a) n", r=4)
+        w_scale3 = w_scale[:].rearrange("p (g n) -> p g n", n=N)
+        for r in range(4):
+            nc.sync.dma_start(w_scale3[r:P:32].bitcast(I32), scale_rows[r].bitcast(I32))
+        bias = keep.tile([P, E], F32, name="bias")
+        nc.sync.dma_start(bias[:], b)
+        token_slots = []
+        for r, pos in enumerate((pos1, pos2, pos3, pos4)):
+            lst = keep.tile([P, T // 16], U16, name="token_slots%d" % r)
+            nc.sync.dma_start(lst[:], pos)
+            token_slots.append(lst)
+
+        in_banks = [banks.tile([P, PACK * P], F32, name="in_bank%d" % i) for i in range(IN_BANKS)]
+        out_banks = [banks.tile([P, PACK * P], F32, name="out_bank%d" % i) for i in range(OUT_BANKS)]
+        stages = [keep.tile([P, PACK * WIDEST], F32, name="stage%d" % i, align_bytes=64) for i in range(STAGES)]
+        gated_tiles = [keep.tile([P, PACK * P], BF16, name="gated%d" % i) for i in range(GATED_TILES)]
+        codes = [keep.tile([P, SLOTS], U32, name="codes%d" % a, align_bytes=64) for a in range(PASSES)]
+        scales = [keep.tile([P, SLOTS], U8, name="scales%d" % a, align_bytes=64) for a in range(PASSES)]
+        y = keep.tile([P, SLOTS], F32, name="y")
+
+        gate_turned = out_banks[OUT_BANKS - 1]
+        nc.tensor.transpose(gate_turned[:, 0:P], gate_rows[:], ident[:])
+        gate_col = keep.tile([P, BLOCKS], F32, name="gate_col")
+        nc.scalar.copy(gate_col[:], gate_turned[:, 0:BLOCKS])
+
+        units = []
+        s0 = 0
+        for width in CHUNKS:
+            units.extend([(s0, width, a) for a in range(PASSES)])
+            s0 = s0 + width
+
+        in_turn = []
+        out_turn = []
+
+        def next_of(tiles, turn):
+            turn.append(0)
+            return tiles[(len(turn) - 1) % len(tiles)]
+
+        def gather(i, planes):
+            s0, width, a = units[i]
+            for j in planes:
+                nc.vector.tensor_copy(
+                    stages[i % STAGES][:, j * WIDEST : j * WIDEST + width],
+                    x_planes[a][j][:].indirect(slot_tokens[:, s0 // 16 : (s0 + width) // 16]),
+                )
+
+        def rounded_words(i):
+            width = units[i][1]
+            return stages[(i - 1) % STAGES][:, 2 * WIDEST : 2 * WIDEST + 2 * width]
+
+        def gate_and_round(i, c0):
+            s0, width, a = units[i]
+            stage = stages[i % STAGES]
+            back = next_of(out_banks, out_turn)
+            for h in range(2):
+                c1 = c0 + h * P
+                turned = next_of(in_banks, in_turn)
+                gated = gated_tiles[(len(in_turn) - 1) % GATED_TILES]
+                for j in range(PACK):
+                    nc.tensor.transpose(
+                        turned[:, j * P : (j + 1) * P], stage[:, j * WIDEST + c1 : j * WIDEST + c1 + P], ident[:]
+                    )
+                col = (s0 + c1) // P
+                nc.scalar.activation(
+                    gated[:].rearrange("s (u p e) -> s u p e", u=2, e=2),
+                    turned[:].rearrange("s (u e p) -> s u p e", u=2, e=2),
+                    ACT.Copy,
+                    scale=gate_col[:, col : col + 1],
+                )
+                gated_words = gated[:].bitcast(F32)
+                for u in range(2):
+                    nc.tensor.transpose(
+                        back[:, (2 * h + u) * P : (2 * h + u + 1) * P], gated_words[:, u * P : (u + 1) * P], ident[:]
+                    )
+            nc.scalar.copy(
+                rounded_words(i)[:, 2 * c0 : 2 * (c0 + C)].rearrange("p (h s u) -> p h s u", h=2, u=2),
+                back[:].rearrange("p (h u s) -> p h s u", h=2, u=2),
+            )
+
+        def quantise(i):
+            s0, width, a = units[i]
+            nc.vector.quantize_mx(
+                out=codes[a][:, s0 : s0 + width].bitcast(FP8X4),
+                scales=scales[a][:, s0 : s0 + width],
+                in_=rounded_words(i).bitcast(BF16),
+            )
+
+        def expert(e):
+            acc = next_of(out_banks, out_turn)
+            for h in range(0, C, P):
+                cols = slice(e * C + h, e * C + h + P)
+                for a in range(PASSES):
+                    g = e * PASSES + a
+                    nc.tensor.matmul_mx(
+                        out=acc[:, h : h + P],
+                        lhsT=w_code[:, g, :].bitcast(FP4X4),
+                        lhsT_scale=w_scale[:, g * N : (g + 1) * N],
+                        rhs=codes[a][:, cols].bitcast(FP8X4),
+                        rhs_scale=scales[a][:, cols],
+                        start=(a == 0),
+                        stop=(a == PASSES - 1),
+                    )
+            nc.scalar.activation(y[:, e * C : (e + 1) * C], acc[:, 0:C], ACT.Silu, bias=bias[:, e : e + 1])
+
+        waiting = []
+        for i in range(STAGES - 2):
+            gather(i, range(PACK))
+        gather(STAGES - 2, range(2))
+        for i in range(len(units)):
+            if i + STAGES - 2 < len(units):
+                gather(i + STAGES - 2, range(2, PACK))
+            if i + STAGES - 1 < len(units):
+                gather(i + STAGES - 1, range(2))
+            s0, width, a = units[i]
+            for c0 in range(0, width, C):
+                gate_and_round(i, c0)
+                if waiting and waiting[0][0] <= i:
+                    expert(waiting.pop(0)[1])
+            quantise(i)
+            if a == PASSES - 1:
+                waiting.extend([(i + EXPERT_LAG, e) for e in range(s0 // C, (s0 + width) // C)])
+        for item in waiting:
+            expert(item[1])
+
+        t0 = 0
+        for width in TOKEN_CUTS:
+            cols = slice(t0 // 16, (t0 + width) // 16)
+            total = keep.tile([P, width], F32, name="total_%d_0" % t0)
+            nc.vector.tensor_copy(total[:], y[:].indirect(token_slots[0][:, cols]))
+            for r in range(1, 4):
+                more = keep.tile([P, width], F32, name="total_%d_%d" % (t0, r))
+                nc.vector.tensor_tensor(more[:], y[:].indirect(token_slots[r][:, cols]), total[:], ADD)
+                total = more
+            nc.sync.dma_start(out[:, t0 : t0 + width], total[:])
+            t0 = t0 + width

@@ -1,22 +1,16 @@
 from contextlib import ExitStack
 
 import concourse.mybir as mybir
-from concourse.masks import make_identity
 
 K, T, E, C, N = 1536, 768, 12, 256, 128
 SLOTS = E * C
 P = 128
 PACK = 4
 PASSES = K // (P * PACK)
-BLOCKS = SLOTS // P
-CHUNKS = (512, 512, 512, 512, 512, 256, 256)
+CHUNKS = (512, 512, 512, 512, 512, 256, 128, 128)
 WIDEST = max(CHUNKS)
-TOKEN_CUTS = (384, 384)
-STAGES = 4
-IN_BANKS = 4
-OUT_BANKS = 4
-GATED_TILES = 4
-EXPERT_LAG = 4
+STAGES = 3
+BANKS = 4
 
 F32 = mybir.dt.float32
 BF16 = mybir.dt.bfloat16
@@ -26,8 +20,9 @@ U16 = mybir.dt.uint16
 U8 = mybir.dt.uint8
 FP8X4 = mybir.dt.float8_e4m3fn_x4
 FP4X4 = mybir.dt.float4_e2m1fn_x4
-ACT = mybir.ActivationFunctionType
+SILU = mybir.ActivationFunctionType.Silu
 ADD = mybir.AluOpType.add
+MULT = mybir.AluOpType.mult
 
 FLOPS = 2 * K * N * SLOTS
 BYTES = 4 * K * T + E * K * N // 2 + E * K * N // 32 + 4 * N * E + 4 * SLOTS + 2 * P * (SLOTS + 4 * T) // 16 + 4 * N * T
@@ -39,29 +34,23 @@ def tile_moe_pre_lin_silu_kernel(
     nc = tc.nc
     with ExitStack() as ctx:
         keep = ctx.enter_context(tc.tile_pool(name="keep", bufs=1))
-        banks = ctx.enter_context(tc.psum_pool(name="banks", bufs=1))
+        psum = ctx.enter_context(tc.psum_pool(name="psum", bufs=1))
 
         slot_tokens = keep.tile([P, SLOTS // 16], U16, name="slot_tokens")
         nc.sync.dma_start(slot_tokens[:], offs)
 
         x_rows = xT.rearrange("(a p j) t -> a j p t", p=P, j=PACK)
         x_planes = [[keep.tile([P, T], F32, name="x_%d_%d" % (a, j)) for j in range(PACK)] for a in range(PASSES)]
-
-        def load_pass(a):
-            for j in range(PACK):
-                nc.sync.dma_start(x_planes[a][j][:], x_rows[a, j])
-
-        ident = keep.tile([P, P], F32, name="ident")
-        make_identity(nc, ident[:])
-        gate_rows = keep.tile([P, P], F32, name="gate_rows")
-        nc.gpsimd.memset(gate_rows[:], 0.0)
+        gate_first = keep.tile([P, CHUNKS[0]], F32, name="gate_first")
+        gate_rest = keep.tile([P, SLOTS - CHUNKS[0]], F32, name="gate_rest")
         w_scale = keep.tile([P, E * PASSES * N], U8, name="w_scale", align_bytes=64)
         nc.gpsimd.memset(w_scale[:].bitcast(I32), 0)
 
-        load_pass(0)
-        nc.sync.dma_start(gate_rows[0:BLOCKS, :], gate[0].rearrange("(b s) -> b s", s=P))
-        load_pass(1)
-        load_pass(2)
+        nc.sync.dma_start(gate_first[:], gate[0:P, 0 : CHUNKS[0]])
+        for a in range(PASSES):
+            for j in range(PACK):
+                nc.sync.dma_start(x_planes[a][j][:], x_rows[a, j])
+        nc.sync.dma_start(gate_rest[:], gate[0:P, CHUNKS[0] : SLOTS])
 
         w_code = keep.tile([P, E * PASSES, 2 * N], U8, name="w_code", align_bytes=64)
         nc.sync.dma_start(w_code[:].bitcast(I32), w_words.rearrange("e a p b -> p (e a) b").bitcast(I32))
@@ -77,18 +66,11 @@ def tile_moe_pre_lin_silu_kernel(
             nc.sync.dma_start(lst[:], pos)
             token_slots.append(lst)
 
-        in_banks = [banks.tile([P, PACK * P], F32, name="in_bank%d" % i) for i in range(IN_BANKS)]
-        out_banks = [banks.tile([P, PACK * P], F32, name="out_bank%d" % i) for i in range(OUT_BANKS)]
+        banks = [psum.tile([P, WIDEST], F32, name="bank%d" % i) for i in range(BANKS)]
         stages = [keep.tile([P, PACK * WIDEST], F32, name="stage%d" % i, align_bytes=64) for i in range(STAGES)]
-        gated_tiles = [keep.tile([P, PACK * P], BF16, name="gated%d" % i) for i in range(GATED_TILES)]
         codes = [keep.tile([P, SLOTS], U32, name="codes%d" % a, align_bytes=64) for a in range(PASSES)]
         scales = [keep.tile([P, SLOTS], U8, name="scales%d" % a, align_bytes=64) for a in range(PASSES)]
         y = keep.tile([P, SLOTS], F32, name="y")
-
-        gate_turned = out_banks[OUT_BANKS - 1]
-        nc.tensor.transpose(gate_turned[:, 0:P], gate_rows[:], ident[:])
-        gate_col = keep.tile([P, BLOCKS], F32, name="gate_col")
-        nc.scalar.copy(gate_col[:], gate_turned[:, 0:BLOCKS])
 
         units = []
         s0 = 0
@@ -96,70 +78,45 @@ def tile_moe_pre_lin_silu_kernel(
             units.extend([(s0, width, a) for a in range(PASSES)])
             s0 = s0 + width
 
-        in_turn = []
-        out_turn = []
-
-        def next_of(tiles, turn):
-            turn.append(0)
-            return tiles[(len(turn) - 1) % len(tiles)]
-
         def gather(i, planes):
             s0, width, a = units[i]
+            weights = gate_first[:] if s0 == 0 else gate_rest[:, s0 - CHUNKS[0] : s0 - CHUNKS[0] + width]
             for j in planes:
-                nc.vector.tensor_copy(
+                nc.vector.tensor_tensor(
                     stages[i % STAGES][:, j * WIDEST : j * WIDEST + width],
                     x_planes[a][j][:].indirect(slot_tokens[:, s0 // 16 : (s0 + width) // 16]),
+                    weights,
+                    MULT,
                 )
 
-        def rounded_words(i):
+        def rounded(i):
             width = units[i][1]
-            return stages[(i - 1) % STAGES][:, 2 * WIDEST : 2 * WIDEST + 2 * width]
+            return stages[(i - 1) % STAGES][:, 2 * WIDEST : 2 * WIDEST + 2 * width].bitcast(BF16)
 
-        def gate_and_round(i, c0):
-            s0, width, a = units[i]
-            stage = stages[i % STAGES]
-            back = next_of(out_banks, out_turn)
-            for h in range(2):
-                c1 = c0 + h * P
-                turned = next_of(in_banks, in_turn)
-                gated = gated_tiles[(len(in_turn) - 1) % GATED_TILES]
-                for j in range(PACK):
-                    nc.tensor.transpose(
-                        turned[:, j * P : (j + 1) * P], stage[:, j * WIDEST + c1 : j * WIDEST + c1 + P], ident[:]
-                    )
-                col = (s0 + c1) // P
-                nc.scalar.activation(
-                    gated[:].rearrange("s (u p e) -> s u p e", u=2, e=2),
-                    turned[:].rearrange("s (u e p) -> s u p e", u=2, e=2),
-                    ACT.Copy,
-                    scale=gate_col[:, col : col + 1],
-                )
-                gated_words = gated[:].bitcast(F32)
-                for u in range(2):
-                    nc.tensor.transpose(
-                        back[:, (2 * h + u) * P : (2 * h + u + 1) * P], gated_words[:, u * P : (u + 1) * P], ident[:]
-                    )
-            nc.scalar.copy(
-                rounded_words(i)[:, 2 * c0 : 2 * (c0 + C)].rearrange("p (h s u) -> p h s u", h=2, u=2),
-                back[:].rearrange("p (h u s) -> p h s u", h=2, u=2),
-            )
+        def round_and_weave(i):
+            width = units[i][1]
+            planes = stages[i % STAGES][:].rearrange("p (j s) -> p j s", j=PACK)[:, :, 0:width]
+            src = planes.rearrange("p j (c n) -> p c j n", n=4)
+            dst = rounded(i).rearrange("p (c n j) -> p c j n", n=4, j=PACK)
+            if i == len(units) - 1:
+                nc.vector.tensor_copy(dst, src)
+            else:
+                nc.scalar.copy(dst, src)
 
         def quantise(i):
             s0, width, a = units[i]
             nc.vector.quantize_mx(
-                out=codes[a][:, s0 : s0 + width].bitcast(FP8X4),
-                scales=scales[a][:, s0 : s0 + width],
-                in_=rounded_words(i).bitcast(BF16),
+                out=codes[a][:, s0 : s0 + width].bitcast(FP8X4), scales=scales[a][:, s0 : s0 + width], in_=rounded(i)
             )
 
-        def expert(e):
-            acc = next_of(out_banks, out_turn)
-            for h in range(0, C, P):
-                cols = slice(e * C + h, e * C + h + P)
+        def experts(s0, width, acc):
+            for c0 in range(0, width, P):
+                e = (s0 + c0) // C
+                cols = slice(s0 + c0, s0 + c0 + P)
                 for a in range(PASSES):
                     g = e * PASSES + a
                     nc.tensor.matmul_mx(
-                        out=acc[:, h : h + P],
+                        out=acc[:, c0 : c0 + P],
                         lhsT=w_code[:, g, :].bitcast(FP4X4),
                         lhsT_scale=w_scale[:, g * N : (g + 1) * N],
                         rhs=codes[a][:, cols].bitcast(FP8X4),
@@ -167,36 +124,36 @@ def tile_moe_pre_lin_silu_kernel(
                         start=(a == 0),
                         stop=(a == PASSES - 1),
                     )
-            nc.scalar.activation(y[:, e * C : (e + 1) * C], acc[:, 0:C], ACT.Silu, bias=bias[:, e : e + 1])
+            piece = min(C, width)
+            for c0 in range(0, width, piece):
+                e = (s0 + c0) // C
+                nc.scalar.activation(
+                    y[:, s0 + c0 : s0 + c0 + piece], acc[:, c0 : c0 + piece], SILU, bias=bias[:, e : e + 1]
+                )
 
-        waiting = []
-        for i in range(STAGES - 2):
-            gather(i, range(PACK))
-        gather(STAGES - 2, range(2))
+        gather(0, range(PACK))
+        gather(1, range(2))
         for i in range(len(units)):
-            if i + STAGES - 2 < len(units):
-                gather(i + STAGES - 2, range(2, PACK))
-            if i + STAGES - 1 < len(units):
-                gather(i + STAGES - 1, range(2))
-            s0, width, a = units[i]
-            for c0 in range(0, width, C):
-                gate_and_round(i, c0)
-                if waiting and waiting[0][0] <= i:
-                    expert(waiting.pop(0)[1])
+            if i + 1 < len(units):
+                gather(i + 1, range(2, PACK))
+            if i + 2 < len(units):
+                gather(i + 2, range(2))
+            round_and_weave(i)
             quantise(i)
+            s0, width, a = units[i]
             if a == PASSES - 1:
-                waiting.extend([(i + EXPERT_LAG, e) for e in range(s0 // C, (s0 + width) // C)])
-        for item in waiting:
-            expert(item[1])
+                experts(s0, width, banks[(i // PASSES) % BANKS])
 
-        t0 = 0
-        for width in TOKEN_CUTS:
-            cols = slice(t0 // 16, (t0 + width) // 16)
-            total = keep.tile([P, width], F32, name="total_%d_0" % t0)
-            nc.vector.tensor_copy(total[:], y[:].indirect(token_slots[0][:, cols]))
-            for r in range(1, 4):
-                more = keep.tile([P, width], F32, name="total_%d_%d" % (t0, r))
-                nc.vector.tensor_tensor(more[:], y[:].indirect(token_slots[r][:, cols]), total[:], ADD)
-                total = more
-            nc.sync.dma_start(out[:, t0 : t0 + width], total[:])
-            t0 = t0 + width
+        half = T // 2
+        totals = [None, None]
+        for r in range(4):
+            for h in range(2):
+                picked = y[:].indirect(token_slots[r][:, h * half // 16 : (h + 1) * half // 16])
+                total = keep.tile([P, half], F32, name="total_%d_%d" % (h, r))
+                if r == 0:
+                    nc.vector.tensor_copy(total[:], picked)
+                else:
+                    nc.vector.tensor_tensor(total[:], picked, totals[h][:], ADD)
+                totals[h] = total
+        for h in range(2):
+            nc.sync.dma_start(out[:, h * half : (h + 1) * half], totals[h][:])

@@ -1,3 +1,4 @@
+import math
 from contextlib import ExitStack
 
 import concourse.mybir as mybir
@@ -7,9 +8,12 @@ SLOTS = E * C
 P = 128
 PACK = 4
 PASSES = K // (P * PACK)
-CHUNKS = (512, 512, 512, 512, 512, 256, 128, 128)
+CHUNKS = (512, 768, 768, 640, 256, 128)
 WIDEST = max(CHUNKS)
-STAGES = 3
+WINDOW = WIDEST + 16
+BANK = 512
+LAST_CUT = 128
+STAGES = 4
 BANKS = 4
 
 F32 = mybir.dt.float32
@@ -40,7 +44,7 @@ def tile_moe_pre_lin_silu_kernel(
         nc.sync.dma_start(slot_tokens[:], offs)
 
         x_rows = xT.rearrange("(a p j) t -> a j p t", p=P, j=PACK)
-        x_planes = [[keep.tile([P, T], F32, name="x_%d_%d" % (a, j)) for j in range(PACK)] for a in range(PASSES)]
+        x_planes = [[keep.tile([P, WINDOW], F32, name="x_%d_%d" % (a, j)) for j in range(PACK)] for a in range(PASSES)]
         gate_first = keep.tile([P, CHUNKS[0]], F32, name="gate_first")
         gate_rest = keep.tile([P, SLOTS - CHUNKS[0]], F32, name="gate_rest")
         w_scale = keep.tile([P, E * PASSES * N], U8, name="w_scale", align_bytes=64)
@@ -49,7 +53,8 @@ def tile_moe_pre_lin_silu_kernel(
         nc.sync.dma_start(gate_first[:], gate[0:P, 0 : CHUNKS[0]])
         for a in range(PASSES):
             for j in range(PACK):
-                nc.sync.dma_start(x_planes[a][j][:], x_rows[a, j])
+                nc.vector.memset(x_planes[a][j][:, T:WINDOW], 0.0)
+                nc.sync.dma_start(x_planes[a][j][:, 0:T], x_rows[a, j])
         nc.sync.dma_start(gate_rest[:], gate[0:P, CHUNKS[0] : SLOTS])
 
         w_code = keep.tile([P, E * PASSES, 2 * N], U8, name="w_code", align_bytes=64)
@@ -66,7 +71,7 @@ def tile_moe_pre_lin_silu_kernel(
             nc.sync.dma_start(lst[:], pos)
             token_slots.append(lst)
 
-        banks = [psum.tile([P, WIDEST], F32, name="bank%d" % i) for i in range(BANKS)]
+        banks = [psum.tile([P, BANK], F32, name="bank%d" % i) for i in range(BANKS)]
         stages = [keep.tile([P, PACK * WIDEST], F32, name="stage%d" % i, align_bytes=64) for i in range(STAGES)]
         codes = [keep.tile([P, SLOTS], U32, name="codes%d" % a, align_bytes=64) for a in range(PASSES)]
         scales = [keep.tile([P, SLOTS], U8, name="scales%d" % a, align_bytes=64) for a in range(PASSES)]
@@ -105,9 +110,16 @@ def tile_moe_pre_lin_silu_kernel(
 
         def quantise(i):
             s0, width, a = units[i]
-            nc.vector.quantize_mx(
-                out=codes[a][:, s0 : s0 + width].bitcast(FP8X4), scales=scales[a][:, s0 : s0 + width], in_=rounded(i)
-            )
+            c0 = 0
+            while c0 < width:
+                part = 1 << int(math.log2(width - c0))
+                cols = slice(s0 + c0, s0 + c0 + part)
+                nc.vector.quantize_mx(
+                    out=codes[a][:, cols].bitcast(FP8X4),
+                    scales=scales[a][:, cols],
+                    in_=rounded(i)[:, PACK * c0 : PACK * (c0 + part)],
+                )
+                c0 = c0 + part
 
         def experts(s0, width, acc):
             for c0 in range(0, width, P):
@@ -124,29 +136,30 @@ def tile_moe_pre_lin_silu_kernel(
                         start=(a == 0),
                         stop=(a == PASSES - 1),
                     )
-            piece = min(C, width)
-            for c0 in range(0, width, piece):
-                e = (s0 + c0) // C
-                nc.scalar.activation(
-                    y[:, s0 + c0 : s0 + c0 + piece], acc[:, c0 : c0 + piece], SILU, bias=bias[:, e : e + 1]
-                )
+            for e in range(s0 // C, (s0 + width - 1) // C + 1):
+                lo, hi = max(s0, e * C), min(s0 + width, (e + 1) * C)
+                nc.scalar.activation(y[:, lo:hi], acc[:, lo - s0 : hi - s0], SILU, bias=bias[:, e : e + 1])
 
-        gather(0, range(PACK))
-        gather(1, range(2))
+        sums = []
+        for i in range(STAGES - 2):
+            gather(i, range(PACK))
+        gather(STAGES - 2, range(2))
         for i in range(len(units)):
-            if i + 1 < len(units):
-                gather(i + 1, range(2, PACK))
-            if i + 2 < len(units):
-                gather(i + 2, range(2))
+            if i + STAGES - 2 < len(units):
+                gather(i + STAGES - 2, range(2, PACK))
+            if i + STAGES - 1 < len(units):
+                gather(i + STAGES - 1, range(2))
             round_and_weave(i)
             quantise(i)
             s0, width, a = units[i]
             if a == PASSES - 1:
-                experts(s0, width, banks[(i // PASSES) % BANKS])
+                for c0 in range(0, width, BANK):
+                    experts(s0 + c0, min(BANK, width - c0), banks[len(sums) % BANKS])
+                    sums.append(s0 + c0)
 
         half = T // 2
         totals = [None, None]
-        for r in range(4):
+        for r in range(3):
             for h in range(2):
                 picked = y[:].indirect(token_slots[r][:, h * half // 16 : (h + 1) * half // 16])
                 total = keep.tile([P, half], F32, name="total_%d_%d" % (h, r))
@@ -155,5 +168,9 @@ def tile_moe_pre_lin_silu_kernel(
                 else:
                     nc.vector.tensor_tensor(total[:], picked, totals[h][:], ADD)
                 totals[h] = total
-        for h in range(2):
-            nc.sync.dma_start(out[:, h * half : (h + 1) * half], totals[h][:])
+        for t0, t1, queue in ((0, half, nc.sync), (half, T - LAST_CUT, nc.scalar), (T - LAST_CUT, T, nc.sync)):
+            h = t0 // half
+            result = keep.tile([P, t1 - t0], F32, name="result_%d" % t0)
+            picked = y[:].indirect(token_slots[3][:, t0 // 16 : t1 // 16])
+            nc.vector.tensor_tensor(result[:], picked, totals[h][:, t0 - h * half : t1 - h * half], ADD)
+            queue.dma_start(out[:, t0:t1], result[:])

import math
from contextlib import ExitStack

import concourse.mybir as mybir

K, T, E, C, N = 1536, 768, 12, 256, 128
SLOTS = E * C
P = 128
PACK = 4
PASSES = K // (P * PACK)
CHUNKS = (512, 768, 768, 640, 256, 128)
WIDEST = max(CHUNKS)
WINDOW = WIDEST + 16
BANK = 512
LAST_CUT = 128
STAGES = 4
BANKS = 4

F32 = mybir.dt.float32
BF16 = mybir.dt.bfloat16
I32 = mybir.dt.int32
U32 = mybir.dt.uint32
U16 = mybir.dt.uint16
U8 = mybir.dt.uint8
FP8X4 = mybir.dt.float8_e4m3fn_x4
FP4X4 = mybir.dt.float4_e2m1fn_x4
SILU = mybir.ActivationFunctionType.Silu
ADD = mybir.AluOpType.add
MULT = mybir.AluOpType.mult

FLOPS = 2 * K * N * SLOTS
BYTES = 4 * K * T + E * K * N // 2 + E * K * N // 32 + 4 * N * E + 4 * SLOTS + 2 * P * (SLOTS + 4 * T) // 16 + 4 * N * T


def tile_moe_pre_lin_silu_kernel(
    tc, xT, w_words, w_scales, b, gate, offs, pos1, pos2, pos3, pos4, out
):
    nc = tc.nc
    with ExitStack() as ctx:
        keep = ctx.enter_context(tc.tile_pool(name="keep", bufs=1))
        psum = ctx.enter_context(tc.psum_pool(name="psum", bufs=1))

        slot_tokens = keep.tile([P, SLOTS // 16], U16, name="slot_tokens")
        nc.sync.dma_start(slot_tokens[:], offs)

        x_rows = xT.rearrange("(a p j) t -> a j p t", p=P, j=PACK)
        x_planes = [[keep.tile([P, WINDOW], F32, name="x_%d_%d" % (a, j)) for j in range(PACK)] for a in range(PASSES)]
        gate_first = keep.tile([P, CHUNKS[0]], F32, name="gate_first")
        gate_rest = keep.tile([P, SLOTS - CHUNKS[0]], F32, name="gate_rest")
        w_scale = keep.tile([P, E * PASSES * N], U8, name="w_scale", align_bytes=64)
        nc.gpsimd.memset(w_scale[:].bitcast(I32), 0)

        nc.sync.dma_start(gate_first[:], gate[0:P, 0 : CHUNKS[0]])
        for a in range(PASSES):
            for j in range(PACK):
                nc.vector.memset(x_planes[a][j][:, T:WINDOW], 0.0)
                nc.sync.dma_start(x_planes[a][j][:, 0:T], x_rows[a, j])
        nc.sync.dma_start(gate_rest[:], gate[0:P, CHUNKS[0] : SLOTS])

        w_code = keep.tile([P, E * PASSES, 2 * N], U8, name="w_code", align_bytes=64)
        nc.sync.dma_start(w_code[:].bitcast(I32), w_words.rearrange("e a p b -> p (e a) b").bitcast(I32))
        scale_rows = w_scales.rearrange("e a (q r) n -> r q (e a) n", r=4)
        w_scale3 = w_scale[:].rearrange("p (g n) -> p g n", n=N)
        for r in range(4):
            nc.sync.dma_start(w_scale3[r:P:32].bitcast(I32), scale_rows[r].bitcast(I32))
        bias = keep.tile([P, E], F32, name="bias")
        nc.sync.dma_start(bias[:], b)
        token_slots = []
        for r, pos in enumerate((pos1, pos2, pos3, pos4)):
            lst = keep.tile([P, T // 16], U16, name="token_slots%d" % r)
            nc.sync.dma_start(lst[:], pos)
            token_slots.append(lst)

        banks = [psum.tile([P, BANK], F32, name="bank%d" % i) for i in range(BANKS)]
        stages = [keep.tile([P, PACK * WIDEST], F32, name="stage%d" % i, align_bytes=64) for i in range(STAGES)]
        codes = [keep.tile([P, SLOTS], U32, name="codes%d" % a, align_bytes=64) for a in range(PASSES)]
        scales = [keep.tile([P, SLOTS], U8, name="scales%d" % a, align_bytes=64) for a in range(PASSES)]
        y = keep.tile([P, SLOTS], F32, name="y")

        units = []
        s0 = 0
        for width in CHUNKS:
            units.extend([(s0, width, a) for a in range(PASSES)])
            s0 = s0 + width

        def gather(i, planes):
            s0, width, a = units[i]
            weights = gate_first[:] if s0 == 0 else gate_rest[:, s0 - CHUNKS[0] : s0 - CHUNKS[0] + width]
            for j in planes:
                nc.vector.tensor_tensor(
                    stages[i % STAGES][:, j * WIDEST : j * WIDEST + width],
                    x_planes[a][j][:].indirect(slot_tokens[:, s0 // 16 : (s0 + width) // 16]),
                    weights,
                    MULT,
                )

        def rounded(i):
            width = units[i][1]
            return stages[(i - 1) % STAGES][:, 2 * WIDEST : 2 * WIDEST + 2 * width].bitcast(BF16)

        def round_and_weave(i):
            width = units[i][1]
            planes = stages[i % STAGES][:].rearrange("p (j s) -> p j s", j=PACK)[:, :, 0:width]
            src = planes.rearrange("p j (c n) -> p c j n", n=4)
            dst = rounded(i).rearrange("p (c n j) -> p c j n", n=4, j=PACK)
            if i == len(units) - 1:
                nc.vector.tensor_copy(dst, src)
            else:
                nc.scalar.copy(dst, src)

        def quantise(i):
            s0, width, a = units[i]
            c0 = 0
            while c0 < width:
                part = 1 << int(math.log2(width - c0))
                cols = slice(s0 + c0, s0 + c0 + part)
                nc.vector.quantize_mx(
                    out=codes[a][:, cols].bitcast(FP8X4),
                    scales=scales[a][:, cols],
                    in_=rounded(i)[:, PACK * c0 : PACK * (c0 + part)],
                )
                c0 = c0 + part

        def experts(s0, width, acc):
            for c0 in range(0, width, P):
                e = (s0 + c0) // C
                cols = slice(s0 + c0, s0 + c0 + P)
                for a in range(PASSES):
                    g = e * PASSES + a
                    nc.tensor.matmul_mx(
                        out=acc[:, c0 : c0 + P],
                        lhsT=w_code[:, g, :].bitcast(FP4X4),
                        lhsT_scale=w_scale[:, g * N : (g + 1) * N],
                        rhs=codes[a][:, cols].bitcast(FP8X4),
                        rhs_scale=scales[a][:, cols],
                        start=(a == 0),
                        stop=(a == PASSES - 1),
                    )
            for e in range(s0 // C, (s0 + width - 1) // C + 1):
                lo, hi = max(s0, e * C), min(s0 + width, (e + 1) * C)
                nc.scalar.activation(y[:, lo:hi], acc[:, lo - s0 : hi - s0], SILU, bias=bias[:, e : e + 1])

        sums = []
        for i in range(STAGES - 2):
            gather(i, range(PACK))
        gather(STAGES - 2, range(2))
        for i in range(len(units)):
            if i + STAGES - 2 < len(units):
                gather(i + STAGES - 2, range(2, PACK))
            if i + STAGES - 1 < len(units):
                gather(i + STAGES - 1, range(2))
            round_and_weave(i)
            quantise(i)
            s0, width, a = units[i]
            if a == PASSES - 1:
                for c0 in range(0, width, BANK):
                    experts(s0 + c0, min(BANK, width - c0), banks[len(sums) % BANKS])
                    sums.append(s0 + c0)

        half = T // 2
        totals = [None, None]
        for r in range(3):
            for h in range(2):
                picked = y[:].indirect(token_slots[r][:, h * half // 16 : (h + 1) * half // 16])
                total = keep.tile([P, half], F32, name="total_%d_%d" % (h, r))
                if r == 0:
                    nc.vector.tensor_copy(total[:], picked)
                else:
                    nc.vector.tensor_tensor(total[:], picked, totals[h][:], ADD)
                totals[h] = total
        for t0, t1, queue in ((0, half, nc.sync), (half, T - LAST_CUT, nc.scalar), (T - LAST_CUT, T, nc.sync)):
            h = t0 // half
            result = keep.tile([P, t1 - t0], F32, name="result_%d" % t0)
            picked = y[:].indirect(token_slots[3][:, t0 // 16 : t1 // 16])
            nc.vector.tensor_tensor(result[:], picked, totals[h][:, t0 - h * half : t1 - h * half], ADD)
            queue.dma_start(out[:, t0:t1], result[:])
